import numpy as np
import ml_dtypes

BF16 = ml_dtypes.bfloat16


def bf(x):
    return np.asarray(x, np.float32).astype(BF16)


def f32(x):
    return np.asarray(x, np.float32)


def f64(x):
    return np.asarray(x).astype(np.float64)


def striped(idx):
    return np.tile(idx.reshape(-1, 16).T, (8, 1))


S, K, M, N, V, D, H = 512, 128, 512, 512, 256, 2, 256


def sigmoid(v):
    return 1.0 / (1.0 + np.exp(-v))


def setup_inputs():
    return {"table": bf(np.random.standard_normal((K, S))), "w": bf(np.random.standard_normal((D, K, M)) / np.sqrt(D * K)), "b": f32(0.5 * np.random.standard_normal((M, 1))), "offs": striped(np.random.permutation(np.tile(np.arange(S), 2))[:N])}


def reference(table, w, b, offs):
    idx = offs[:16].T.reshape(-1)
    x = f64(table)[:, idx]
    y = sum(f64(w)[t].T @ x[:, t * V : (t + 1) * V] for t in range(D)) + f64(b)
    return sigmoid(y[:H]) * np.maximum(y[H:], 0.0)

@@ -1,0 +1,52 @@
+import concourse.mybir as mybir
+
+P = 128
+NODES = 512
+EDGES = 256
+ENDS = 2
+ROWS = 512
+HALF = ROWS // 2
+LIST_COLS = EDGES // 16
+
+FLOPS = 2 * ENDS * P * ROWS * EDGES
+
+BF16, F32, U16 = mybir.dt.bfloat16, mybir.dt.float32, mybir.dt.uint16
+ALU = mybir.AluOpType
+ACT = mybir.ActivationFunctionType
+
+
+def tile_rows_ggate_relu_rep_kernel(tc, table, w, b, offs, out):
+    nc = tc.nc
+    with (
+        tc.tile_pool(name="held", bufs=1) as held,
+        tc.psum_pool(name="psum", bufs=1) as psum,
+    ):
+        offsets = held.tile([P, ENDS * LIST_COLS], U16)
+        nodes = held.tile([P, NODES], BF16)
+        weights = held.tile([P, ENDS, ROWS], BF16)
+        bias = held.tile([P, ROWS // P], F32)
+        nc.sync.dma_start(offsets[:], offs)
+        nc.sync.dma_start(nodes[:], table)
+        nc.scalar.dma_start(weights[:], w.rearrange("t k m -> k t m"))
+        nc.scalar.dma_start(bias[:], b.rearrange("(a p) o -> p (a o)", p=P))
+
+        def rows_of_y(block):
+            bank = psum.tile([P, EDGES], F32, name=f"y{block}")
+            for t in range(ENDS):
+                picked = nodes[:].indirect(offsets[:, t * LIST_COLS : (t + 1) * LIST_COLS])
+                nc.tensor.matmul(bank[:], weights[:, t, block * P : (block + 1) * P], picked,
+                                 start=(t == 0), stop=(t == ENDS - 1))
+            return bank
+
+        for block in range(HALF // P):
+            value_block = HALF // P + block
+            value_sum = rows_of_y(value_block)
+            gate_sum = rows_of_y(block)
+            value = held.tile([P, EDGES], F32, name=f"value{block}")
+            gate = held.tile([P, EDGES], F32, name=f"gate{block}")
+            message = held.tile([P, EDGES], F32, name=f"message{block}")
+            nc.vector.tensor_scalar(value[:], value_sum[:], bias[:, value_block : value_block + 1], 0.0,
+                                    ALU.add, ALU.max)
+            nc.scalar.activation(gate[:], gate_sum[:], ACT.Sigmoid, bias=bias[:, block : block + 1])
+            nc.vector.tensor_tensor(message[:], value[:], gate[:], ALU.mult)
+            nc.sync.dma_start(out[block * P : (block + 1) * P, :], message[:])

@@ -23,25 +23,28 @@ def tile_rows_ggate_relu_rep_kernel(tc, table, w, b, offs, out):
     ):
         offsets = held.tile([P, ENDS * LIST_COLS], U16)
         nodes = held.tile([P, NODES], BF16)
-        weights = held.tile([P, ENDS, ROWS], BF16)
+        weights = [held.tile([P, ROWS], BF16, name=f"weights{t}") for t in range(ENDS)]
         bias = held.tile([P, ROWS // P], F32)
-        nc.sync.dma_start(offsets[:], offs)
         nc.sync.dma_start(nodes[:], table)
-        nc.scalar.dma_start(weights[:], w.rearrange("t k m -> k t m"))
+        nc.scalar.dma_start(weights[0][:], w[0])
+        nc.sync.dma_start(offsets[:], offs)
+        nc.sync.dma_start(weights[1][:], w[1])
         nc.scalar.dma_start(bias[:], b.rearrange("(a p) o -> p (a o)", p=P))
 
-        def rows_of_y(block):
-            bank = psum.tile([P, EDGES], F32, name=f"y{block}")
-            for t in range(ENDS):
-                picked = nodes[:].indirect(offsets[:, t * LIST_COLS : (t + 1) * LIST_COLS])
-                nc.tensor.matmul(bank[:], weights[:, t, block * P : (block + 1) * P], picked,
-                                 start=(t == 0), stop=(t == ENDS - 1))
-            return bank
+        warm = held.tile([P, 1], F32)
+        warm_out = held.tile([P, 1], F32)
+        nc.vector.memset(warm[:], 0.0)
+        nc.scalar.activation(warm_out[:], warm[:], ACT.Sigmoid)
 
         for block in range(HALF // P):
             value_block = HALF // P + block
-            value_sum = rows_of_y(value_block)
-            gate_sum = rows_of_y(block)
+            value_sum = psum.tile([P, EDGES], F32, name=f"value_sum{block}")
+            gate_sum = psum.tile([P, EDGES], F32, name=f"gate_sum{block}")
+            for t in range(ENDS):
+                picked = nodes[:].indirect(offsets[:, t * LIST_COLS : (t + 1) * LIST_COLS])
+                for bank, rows in ((value_sum, value_block), (gate_sum, block)):
+                    nc.tensor.matmul(bank[:], weights[t][:, rows * P : (rows + 1) * P], picked,
+                                     start=(t == 0), stop=(t == ENDS - 1))
             value = held.tile([P, EDGES], F32, name=f"value{block}")
             gate = held.tile([P, EDGES], F32, name=f"gate{block}")
             message = held.tile([P, EDGES], F32, name=f"message{block}")

@@ -8,6 +8,8 @@ ROWS = 512
 HALF = ROWS // 2
 LIST_COLS = EDGES // 16
 
+WARM_MATMULS = 16
+
 FLOPS = 2 * ENDS * P * ROWS * EDGES
 
 BF16, F32, U16 = mybir.dt.bfloat16, mybir.dt.float32, mybir.dt.uint16
@@ -31,25 +33,39 @@ def tile_rows_ggate_relu_rep_kernel(tc, table, w, b, offs, out):
         nc.sync.dma_start(weights[1][:], w[1])
         nc.scalar.dma_start(bias[:], b.rearrange("(a p) o -> p (a o)", p=P))
 
-        warm = held.tile([P, 1], F32)
-        warm_out = held.tile([P, 1], F32)
-        nc.vector.memset(warm[:], 0.0)
-        nc.scalar.activation(warm_out[:], warm[:], ACT.Sigmoid)
+        zeros = held.tile([P, P], BF16)
+        warm_gate = held.tile([P, 1], F32)
+        warm_sum = psum.tile([P, P], F32)
+        nc.vector.memset(zeros[:], 0.0)
+        nc.scalar.activation(warm_gate[:], zeros[:, :1], ACT.Sigmoid)
+        for step in range(WARM_MATMULS):
+            nc.tensor.matmul(warm_sum[:], zeros[:, :P], zeros[:], start=True, stop=True)
 
-        for block in range(HALF // P):
-            value_block = HALF // P + block
+        def end_term(bank, t, rows, first, count):
+            column = (t * EDGES + first) // 16
+            picked = nodes[:].indirect(offsets[:, column : column + count // 16])
+            nc.tensor.matmul(bank[:], weights[t][:, rows * P : (rows + 1) * P], picked,
+                             start=(t == 0), stop=(t == ENDS - 1))
+
+        blocks = HALF // P
+        for block in range(blocks):
+            value_block = blocks + block
+            width = EDGES // 2 if block == blocks - 1 else EDGES
+            firsts = range(0, EDGES, width)
             value_sum = psum.tile([P, EDGES], F32, name=f"value_sum{block}")
-            gate_sum = psum.tile([P, EDGES], F32, name=f"gate_sum{block}")
+            gate_sums = [psum.tile([P, width], F32, name=f"gate_sum{block}_{first}") for first in firsts]
             for t in range(ENDS):
-                picked = nodes[:].indirect(offsets[:, t * LIST_COLS : (t + 1) * LIST_COLS])
-                for bank, rows in ((value_sum, value_block), (gate_sum, block)):
-                    nc.tensor.matmul(bank[:], weights[t][:, rows * P : (rows + 1) * P], picked,
-                                     start=(t == 0), stop=(t == ENDS - 1))
+                end_term(value_sum, t, value_block, 0, EDGES)
+                end_term(gate_sums[0], t, block, 0, width)
+            for first, gate_sum in zip(firsts[1:], gate_sums[1:]):
+                for t in range(ENDS):
+                    end_term(gate_sum, t, block, first, width)
             value = held.tile([P, EDGES], F32, name=f"value{block}")
-            gate = held.tile([P, EDGES], F32, name=f"gate{block}")
-            message = held.tile([P, EDGES], F32, name=f"message{block}")
             nc.vector.tensor_scalar(value[:], value_sum[:], bias[:, value_block : value_block + 1], 0.0,
                                     ALU.add, ALU.max)
-            nc.scalar.activation(gate[:], gate_sum[:], ACT.Sigmoid, bias=bias[:, block : block + 1])
-            nc.vector.tensor_tensor(message[:], value[:], gate[:], ALU.mult)
-            nc.sync.dma_start(out[block * P : (block + 1) * P, :], message[:])
+            for first, gate_sum in zip(firsts, gate_sums):
+                gate = held.tile([P, width], F32, name=f"gate{block}_{first}")
+                message = held.tile([P, width], F32, name=f"message{block}_{first}")
+                nc.scalar.activation(gate[:], gate_sum[:], ACT.Sigmoid, bias=bias[:, block : block + 1])
+                nc.vector.tensor_tensor(message[:], value[:, first : first + width], gate[:], ALU.mult)
+                nc.sync.dma_start(out[block * P : (block + 1) * P, first : first + width], message[:])

import concourse.mybir as mybir

P = 128
NODES = 512
EDGES = 256
ENDS = 2
ROWS = 512
HALF = ROWS // 2
LIST_COLS = EDGES // 16

WARM_MATMULS = 16

FLOPS = 2 * ENDS * P * ROWS * EDGES

BF16, F32, U16 = mybir.dt.bfloat16, mybir.dt.float32, mybir.dt.uint16
ALU = mybir.AluOpType
ACT = mybir.ActivationFunctionType


def tile_rows_ggate_relu_rep_kernel(tc, table, w, b, offs, out):
    nc = tc.nc
    with (
        tc.tile_pool(name="held", bufs=1) as held,
        tc.psum_pool(name="psum", bufs=1) as psum,
    ):
        offsets = held.tile([P, ENDS * LIST_COLS], U16)
        nodes = held.tile([P, NODES], BF16)
        weights = [held.tile([P, ROWS], BF16, name=f"weights{t}") for t in range(ENDS)]
        bias = held.tile([P, ROWS // P], F32)
        nc.sync.dma_start(nodes[:], table)
        nc.scalar.dma_start(weights[0][:], w[0])
        nc.sync.dma_start(offsets[:], offs)
        nc.sync.dma_start(weights[1][:], w[1])
        nc.scalar.dma_start(bias[:], b.rearrange("(a p) o -> p (a o)", p=P))

        zeros = held.tile([P, P], BF16)
        warm_gate = held.tile([P, 1], F32)
        warm_sum = psum.tile([P, P], F32)
        nc.vector.memset(zeros[:], 0.0)
        nc.scalar.activation(warm_gate[:], zeros[:, :1], ACT.Sigmoid)
        for step in range(WARM_MATMULS):
            nc.tensor.matmul(warm_sum[:], zeros[:, :P], zeros[:], start=True, stop=True)

        def end_term(bank, t, rows, first, count):
            column = (t * EDGES + first) // 16
            picked = nodes[:].indirect(offsets[:, column : column + count // 16])
            nc.tensor.matmul(bank[:], weights[t][:, rows * P : (rows + 1) * P], picked,
                             start=(t == 0), stop=(t == ENDS - 1))

        blocks = HALF // P
        for block in range(blocks):
            value_block = blocks + block
            width = EDGES // 2 if block == blocks - 1 else EDGES
            firsts = range(0, EDGES, width)
            value_sum = psum.tile([P, EDGES], F32, name=f"value_sum{block}")
            gate_sums = [psum.tile([P, width], F32, name=f"gate_sum{block}_{first}") for first in firsts]
            for t in range(ENDS):
                end_term(value_sum, t, value_block, 0, EDGES)
                end_term(gate_sums[0], t, block, 0, width)
            for first, gate_sum in zip(firsts[1:], gate_sums[1:]):
                for t in range(ENDS):
                    end_term(gate_sum, t, block, first, width)
            value = held.tile([P, EDGES], F32, name=f"value{block}")
            nc.vector.tensor_scalar(value[:], value_sum[:], bias[:, value_block : value_block + 1], 0.0,
                                    ALU.add, ALU.max)
            for first, gate_sum in zip(firsts, gate_sums):
                gate = held.tile([P, width], F32, name=f"gate{block}_{first}")
                message = held.tile([P, width], F32, name=f"message{block}_{first}")
                nc.scalar.activation(gate[:], gate_sum[:], ACT.Sigmoid, bias=bias[:, block : block + 1])
                nc.vector.tensor_tensor(message[:], value[:, first : first + width], gate[:], ALU.mult)
                nc.sync.dma_start(out[block * P : (block + 1) * P, first : first + width], message[:])
